import numpy as np
import ml_dtypes


def mxq(x, axis, fmt="e4m3"):
    dtype, down = {"e4m3": (ml_dtypes.float8_e4m3fn, 7), "e5m2": (ml_dtypes.float8_e5m2, 14)}[fmt]
    v = np.moveaxis(np.asarray(x, np.float32).astype(ml_dtypes.bfloat16).astype(np.float64), axis, -1)
    blocks = v.reshape(v.shape[:-1] + (-1, 32))
    amax = np.abs(blocks).max(-1, keepdims=True)
    byte = np.maximum(np.where(amax > 0, np.frexp(amax)[1] - 1 + 127, 0) - down, 1)
    scale = np.exp2(byte - 127.0)
    codes = (blocks / scale).astype(np.float32).astype(dtype).astype(np.float64)
    return np.moveaxis((codes * scale).reshape(v.shape), -1, axis)


WIDE = False


def mx_kscale(k):
    if not WIDE:
        return np.ones(k)
    levels = np.array([30, -30])
    if k % 512:
        return np.exp2(np.random.permutation(np.resize(levels, k // 32))).repeat(32)
    a = np.empty((k // 512, 16))
    for p in range(k // 512):
        a[p, :8] = np.random.permutation(np.resize(levels, 8))
        for g in range(8):
            far = levels[np.abs(levels - a[p, g]) >= 10]
            a[p, g + 8] = far[np.random.randint(len(far))]
    return np.exp2(a.ravel()).repeat(32)


def f64(x):
    return np.asarray(x).astype(np.float64)


def striped(idx):
    return np.tile(np.asarray(idx).reshape(-1, 16).T, (8, 1)).astype(np.uint16)


def unstriped(offs):
    return offs[:16].T.reshape(-1).astype(np.int64)


E2M1 = np.array([0.0, 0.5, 1.0, 1.5, 2.0, 3.0, 4.0, 6.0, -0.0, -0.5, -1.0, -1.5, -2.0, -3.0, -4.0, -6.0])


def pack_weight(w, fmt):
    k, n = w.shape
    w = f64(np.asarray(w, np.float32).astype(ml_dtypes.bfloat16)).reshape(k // 32, 32, n)
    amax = np.abs(w).max(1)
    if fmt == "e4m3":
        byte = np.frexp(amax)[1] - 1 + 127 - 7
    else:
        mant, ex = np.frexp(amax / 6.0)
        byte = np.where(mant > 0.5, ex, ex - 1) + 127
    byte = np.clip(np.where(amax > 0, byte, 1), 1, 254)
    scaled = (w * np.exp2(127.0 - byte)[:, None, :]).reshape(k, n).astype(np.float32)
    by_word = np.ascontiguousarray(scaled.reshape(k // 512, 128, 4, n).transpose(0, 1, 3, 2))
    if fmt == "e4m3":
        words = by_word.astype(ml_dtypes.float8_e4m3fn).view(np.uint8)
    else:
        c = by_word.astype(ml_dtypes.float4_e2m1fn).view(np.uint8) & 0xF
        words = (c[..., 0::2] | (c[..., 1::2] << 4)).reshape(k // 512, 128, 2 * n)
    return np.ascontiguousarray(words), np.ascontiguousarray(byte.astype(np.uint8).reshape(k // 512, 16, n))


def unpack_weight(words, scales, fmt):
    g, _, n = scales.shape
    words = np.ascontiguousarray(words).reshape(g, 128, n, -1)
    if fmt == "e4m3":
        vals = words.view(ml_dtypes.float8_e4m3fn).astype(np.float64)
    else:
        nib = np.empty((g, 128, n, 4), np.uint8)
        nib[..., 0::2] = words & 0xF
        nib[..., 1::2] = words >> 4
        vals = E2M1[nib]
    vals = vals * np.repeat(np.exp2(scales.astype(np.float64) - 127.0), 8, axis=1)[..., None]
    return vals.transpose(0, 1, 3, 2).reshape(g * 512, n)


K, F, T, Z, J, R, O, N = 512, 512, 1024, 1024, 256, 512, 128, 256


def setup_inputs():
    n = np.random.standard_normal
    idx = np.random.permutation(T)[:J]
    idx2 = np.random.permutation(Z)[:J]
    idx3 = np.random.permutation(J)[:O]
    idx4 = np.random.permutation(J)[:O]
    idx5 = np.random.permutation(T)[:O]
    fk = mx_kscale(K)
    fr = mx_kscale(R)
    ff = mx_kscale(F)
    xtp = pack_weight(n((K, T)) / fk[:, None], "e2m1")
    wp = pack_weight(n((K, R)) * 1 / np.sqrt(K) * fk[:, None] * fr, "e4m3")
    xop = pack_weight(n((F, Z)) / ff[:, None], "e4m3")
    w2p = pack_weight(n((F, R)) * 1 / np.sqrt(F) * ff[:, None] * fr, "e2m1")
    wbp = pack_weight(n((R, N)) * 1 / np.sqrt(R) / fr[:, None], "e2m1")
    wsp = pack_weight(n((K, N)) * 1 / np.sqrt(K) * fk[:, None], "e4m3")
    return {
        "xt_words": xtp[0],
        "xt_scales": xtp[1],
        "w_words": wp[0],
        "w_scales": wp[1],
        "xo_words": xop[0],
        "xo_scales": xop[1],
        "w2_words": w2p[0],
        "w2_scales": w2p[1],
        "sa": (np.random.uniform(0.5, 1.6, (R, 1))).astype(np.float32),
        "sb": (np.random.uniform(0.5, 1.6, (R, 1))).astype(np.float32),
        "wb_words": wbp[0],
        "wb_scales": wbp[1],
        "ws_words": wsp[0],
        "ws_scales": wsp[1],
        "offs": striped(idx),
        "offs2": striped(idx2),
        "offs3": striped(idx3),
        "offs4": striped(idx4),
        "offs5": striped(idx5),
    }


def reference(xt_words, xt_scales, w_words, w_scales, xo_words, xo_scales, w2_words, w2_scales, sa, sb, wb_words, wb_scales, ws_words, ws_scales, offs, offs2, offs3, offs4, offs5):
    idx = unstriped(offs)
    idx2 = unstriped(offs2)
    idx3 = unstriped(offs3)
    idx4 = unstriped(offs4)
    idx5 = unstriped(offs5)
    xtu = unpack_weight(xt_words, xt_scales, "e2m1")
    wu = unpack_weight(w_words, w_scales, "e4m3")
    xou = unpack_weight(xo_words, xo_scales, "e4m3")
    w2u = unpack_weight(w2_words, w2_scales, "e2m1")
    wbu = unpack_weight(wb_words, wb_scales, "e2m1")
    wsu = unpack_weight(ws_words, ws_scales, "e4m3")
    xtidxg = xtu[:, idx]
    a = wu.T @ xtidxg
    xoidx2g = xou[:, idx2]
    b = w2u.T @ xoidx2g
    hid = np.abs(a[:, idx3] * f64(sa) - b[:, idx4] * f64(sb))
    hidq = mxq(hid, 0, "e5m2")
    xtidx5g = xtu[:, idx5]
    y = wbu.T @ hidq + wsu.T @ xtidx5g
    return y

@@ -1,0 +1,190 @@
+from contextlib import ExitStack
+
+import concourse.mybir as mybir
+
+K, F, T, Z, J, R, O, N = 512, 512, 1024, 1024, 256, 512, 128, 256
+FLOPS = 2 * (K * R * J + F * R * J + R * N * O + K * N * O)
+
+F32 = mybir.dt.float32
+BF16 = mybir.dt.bfloat16
+I32 = mybir.dt.int32
+U32 = mybir.dt.uint32
+U16 = mybir.dt.uint16
+U8 = mybir.dt.uint8
+E4M3 = mybir.dt.float8_e4m3fn_x4
+E5M2 = mybir.dt.float8_e5m2_x4
+E2M1 = mybir.dt.float4_e2m1fn_x4
+ACT = mybir.ActivationFunctionType
+ALU = mybir.AluOpType
+
+P = 128
+PACK = 4
+QUADS = 4
+QUAD = 32
+ROWS = 4
+
+
+def tile_list_weighedboth_twotab_further_plain_kernel(
+    tc, xt_words, xt_scales, w_words, w_scales, xo_words, xo_scales, w2_words, w2_scales, sa, sb,
+    wb_words, wb_scales, ws_words, ws_scales, offs, offs2, offs3, offs4, offs5, out,
+):
+    nc = tc.nc
+    with ExitStack() as ctx:
+        sb_pool = ctx.enter_context(tc.tile_pool(name="sbuf", bufs=1))
+        psum = ctx.enter_context(tc.psum_pool(name="psum", bufs=1))
+
+        def tile(name, cols, dtype, parts=P):
+            return sb_pool.tile([parts, cols], dtype, name=name, align_bytes=64)
+
+        def load_list(name, src):
+            t = sb_pool.tile(list(src.shape), U16, name=name)
+            nc.sync.dma_start(t[:], src)
+            return t
+
+        def zeroed_plane(name, cols):
+            t = tile(name, cols, U8)
+            nc.vector.memset(t[:].bitcast(I32), 0)
+            return t
+
+        def load_plane(plane, scales):
+            rows = scales[0].bitcast(I32)
+            for q in range(QUADS):
+                nc.sync.dma_start(plane[QUAD * q : QUAD * q + ROWS, :].bitcast(I32), rows[ROWS * q : ROWS * (q + 1), :])
+
+        def load_staged(name, scales):
+            cols = scales.shape[2] // 4
+            t = sb_pool.tile([ROWS, QUADS, cols], I32, name=name)
+            nc.sync.dma_start(t[:], scales[0].bitcast(I32).rearrange("(q r) c -> r q c", r=ROWS))
+            return t
+
+        def spread(plane, staged):
+            for q in range(QUADS):
+                nc.vector.tensor_copy(plane[QUAD * q : QUAD * q + ROWS, :].bitcast(I32), staged[:, q, :])
+
+        def deal_bytes(name, plane):
+            t = tile(name, R, U8)
+            nc.vector.tensor_copy(t[:].rearrange("p (t m) -> p t m", t=PACK), plane[:].rearrange("p (m t) -> p t m", t=PACK))
+            return t
+
+        def gather(name, window, offsets, n, dtype):
+            t = tile(name, n, dtype)
+            nc.vector.tensor_copy(t[:], window.indirect(offsets[:]))
+            return t
+
+        xt_plane = zeroed_plane("xt_plane", T)
+        w_plane = zeroed_plane("w_plane", R)
+        xo_plane = zeroed_plane("xo_plane", Z)
+        w2_plane = zeroed_plane("w2_plane", R)
+        ws_plane = zeroed_plane("ws_plane", N)
+        wb_plane = zeroed_plane("wb_plane", N)
+
+        xt = tile("xt", T, U16)
+        nc.scalar.dma_start(xt[:].bitcast(I32), xt_words[0].bitcast(I32))
+        w = tile("w", R, I32)
+        nc.scalar.dma_start(w[:], w_words[0].rearrange("p n t -> p (n t)").bitcast(I32))
+        sa_t = tile("sa_t", PACK, F32)
+        nc.gpsimd.dma_start(sa_t[:], sa.rearrange("(p t) o -> p (t o)", t=PACK))
+        sb_t = tile("sb_t", PACK, F32)
+        nc.gpsimd.dma_start(sb_t[:], sb.rearrange("(p t) o -> p (t o)", t=PACK))
+
+        l1 = load_list("l1", offs)
+        w_staged = load_staged("w_staged", w_scales)
+        load_plane(xt_plane, xt_scales)
+        w2 = tile("w2", R, U16)
+        nc.sync.dma_start(w2[:].bitcast(I32), w2_words[0].bitcast(I32))
+        xo = tile("xo", Z, I32)
+        nc.sync.dma_start(xo[:], xo_words[0].rearrange("p n t -> p (n t)").bitcast(I32))
+        l2 = load_list("l2", offs2)
+        w2_staged = load_staged("w2_staged", w2_scales)
+        load_plane(xo_plane, xo_scales)
+        l3 = load_list("l3", offs3)
+        l5 = load_list("l5", offs5)
+        l4 = load_list("l4", offs4)
+        ws = tile("ws", N, I32)
+        nc.sync.dma_start(ws[:], ws_words[0].rearrange("p n t -> p (n t)").bitcast(I32))
+        wb = tile("wb", N, U16)
+        nc.sync.dma_start(wb[:].bitcast(I32), wb_words[0].bitcast(I32))
+        load_plane(ws_plane, ws_scales)
+        load_plane(wb_plane, wb_scales)
+
+        w_dealt = tile("w_dealt", R, U32)
+        nc.scalar.copy(w_dealt[:].rearrange("p (t m) -> p m t", t=PACK), w[:].bitcast(U32).rearrange("p (m t) -> p m t", t=PACK))
+        spread(w_plane, w_staged)
+        w_sc = deal_bytes("w_sc", w_plane)
+        xt_sc = gather("xt_sc", xt_plane[:], l1, J, U8)
+        xt_g = gather("xt_g", xt[:], l1, J, U16)
+        w2_dealt = tile("w2_dealt", R, U16)
+        nc.scalar.copy(w2_dealt[:].rearrange("p (t m) -> p t m", t=PACK), w2[:].rearrange("p (m t) -> p t m", t=PACK))
+
+        a_ps = []
+        for t in range(PACK):
+            cols = slice(P * t, P * (t + 1))
+            ps = psum.tile([P, J], F32, name="a_ps%d" % t, tag="bank%d" % t)
+            nc.tensor.matmul_mx(out=ps[:], lhsT=w_dealt[:, cols].bitcast(E4M3), lhsT_scale=w_sc[:, cols],
+                                rhs=xt_g[:].bitcast(E2M1), rhs_scale=xt_sc[:], start=True, stop=True)
+            a_ps.append(ps)
+
+        spread(w2_plane, w2_staged)
+        w2_sc = deal_bytes("w2_sc", w2_plane)
+        xo_sc = gather("xo_sc", xo_plane[:], l2, J, U8)
+        xo_g = gather("xo_g", xo[:].bitcast(U32), l2, J, U32)
+
+        ga = sb_pool.tile([P, PACK, O], F32, name="ga")
+        gb = sb_pool.tile([P, PACK, O], F32, name="gb")
+        a_sb = []
+        for t in range(PACK):
+            a_t = tile("a%d" % t, J, F32)
+            nc.scalar.copy(a_t[:], a_ps[t][:])
+            a_sb.append(a_t)
+            if t > 0:
+                nc.scalar.activation(out=ga[:, t - 1, :], in_=a_sb[t - 1][:].indirect(l3[:]), func=ACT.Copy, scale=sa_t[:, t - 1 : t])
+        nc.scalar.activation(out=ga[:, PACK - 1, :], in_=a_sb[PACK - 1][:].indirect(l3[:]), func=ACT.Copy, scale=sa_t[:, PACK - 1 : PACK])
+
+        b_ps = []
+        for t in range(PACK):
+            cols = slice(P * t, P * (t + 1))
+            ps = psum.tile([P, J], F32, name="b_ps%d" % t, tag="bank%d" % (PACK + t))
+            nc.tensor.matmul_mx(out=ps[:], lhsT=w2_dealt[:, cols].bitcast(E2M1), lhsT_scale=w2_sc[:, cols],
+                                rhs=xo_g[:].bitcast(E4M3), rhs_scale=xo_sc[:], start=True, stop=True)
+            b_ps.append(ps)
+
+        x5_sc = gather("x5_sc", xt_plane[:], l5, O, U8)
+        x5_g = gather("x5_g", xt[:], l5, O, U16)
+
+        diff = sb_pool.tile([P, PACK, O], F32, name="diff")
+        for t in range(PACK):
+            b_t = tile("b%d" % t, J, F32)
+            nc.vector.tensor_copy(b_t[:], b_ps[t][:])
+            nc.scalar.activation(out=gb[:, t, :], in_=b_t[:].indirect(l4[:]), func=ACT.Copy, scale=sb_t[:, t : t + 1])
+
+        y_ps = []
+        for u in range(N // P):
+            cols = slice(P * u, P * (u + 1))
+            ps = psum.tile([P, O], F32, name="y_ps%d" % u, tag="bank%d" % u)
+            nc.tensor.matmul_mx(out=ps[:], lhsT=ws[:, cols].bitcast(E4M3), lhsT_scale=ws_plane[:, cols],
+                                rhs=x5_g[:].bitcast(E2M1), rhs_scale=x5_sc[:], start=True, stop=False)
+            y_ps.append(ps)
+
+        for t in range(PACK):
+            nc.vector.tensor_tensor(diff[:, t, :], ga[:, t, :], gb[:, t, :], ALU.subtract)
+
+        hid = sb_pool.tile([P, O, PACK], BF16, name="hid", align_bytes=64)
+        diff_ot = diff[:].rearrange("p t o -> p o t")
+        half = O // 2
+        nc.vector.scalar_tensor_tensor(hid[:, :half, :], diff_ot[:, :half, :], -1.0, diff_ot[:, :half, :], ALU.mult, ALU.max)
+        nc.scalar.activation(out=hid[:, half:, :], in_=diff_ot[:, half:, :], func=ACT.Abs)
+
+        hid_q = tile("hid_q", O, U32)
+        hid_sc = tile("hid_sc", O, U8)
+        nc.vector.quantize_mx(out=hid_q[:].bitcast(E5M2), scales=hid_sc[:], in_=hid[:].rearrange("p o t -> p (o t)"))
+
+        for u in range(N // P):
+            cols = slice(P * u, P * (u + 1))
+            nc.tensor.matmul_mx(out=y_ps[u][:], lhsT=wb[:, cols].bitcast(E2M1), lhsT_scale=wb_plane[:, cols],
+                                rhs=hid_q[:].bitcast(E5M2), rhs_scale=hid_sc[:], start=False, stop=True)
+        y0 = tile("y0", O, F32)
+        nc.vector.tensor_copy(y0[:], y_ps[0][:])
+        nc.sync.dma_start(out[0:P, :], y0[:])
+        y1 = tile("y1", O, F32)
+        nc.scalar.copy(y1[:], y_ps[1][:])
+        nc.scalar.dma_start(out[P:N, :], y1[:])

@@ -41,20 +41,20 @@ def tile_list_weighedboth_twotab_further_plain_kernel(
             nc.sync.dma_start(t[:], src)
             return t
 
-        def zeroed_plane(name, cols):
+        def zeroed_plane(name, cols, engine):
             t = tile(name, cols, U8)
-            nc.vector.memset(t[:].bitcast(I32), 0)
+            engine.memset(t[:].bitcast(I32), 0)
             return t
 
-        def load_plane(plane, scales):
+        def load_plane(plane, scales, queue):
             rows = scales[0].bitcast(I32)
             for q in range(QUADS):
-                nc.sync.dma_start(plane[QUAD * q : QUAD * q + ROWS, :].bitcast(I32), rows[ROWS * q : ROWS * (q + 1), :])
+                queue.dma_start(plane[QUAD * q : QUAD * q + ROWS, :].bitcast(I32), rows[ROWS * q : ROWS * (q + 1), :])
 
-        def load_staged(name, scales):
+        def load_staged(name, scales, queue):
             cols = scales.shape[2] // 4
             t = sb_pool.tile([ROWS, QUADS, cols], I32, name=name)
-            nc.sync.dma_start(t[:], scales[0].bitcast(I32).rearrange("(q r) c -> r q c", r=ROWS))
+            queue.dma_start(t[:], scales[0].bitcast(I32).rearrange("(q r) c -> r q c", r=ROWS))
             return t
 
         def spread(plane, staged):
@@ -71,47 +71,47 @@ def tile_list_weighedboth_twotab_further_plain_kernel(
             nc.vector.tensor_copy(t[:], window.indirect(offsets[:]))
             return t
 
-        xt_plane = zeroed_plane("xt_plane", T)
-        w_plane = zeroed_plane("w_plane", R)
-        xo_plane = zeroed_plane("xo_plane", Z)
-        w2_plane = zeroed_plane("w2_plane", R)
-        ws_plane = zeroed_plane("ws_plane", N)
-        wb_plane = zeroed_plane("wb_plane", N)
+        xt_plane = zeroed_plane("xt_plane", T, nc.vector)
+        w_plane = zeroed_plane("w_plane", R, nc.vector)
+        xo_plane = zeroed_plane("xo_plane", Z, nc.vector)
+        w2_plane = zeroed_plane("w2_plane", R, nc.vector)
+        ws_plane = zeroed_plane("ws_plane", N, nc.vector)
+        wb_plane = zeroed_plane("wb_plane", N, nc.vector)
 
+        xt_staged = load_staged("xt_staged", xt_scales, nc.sync)
+        w_staged = load_staged("w_staged", w_scales, nc.sync)
         xt = tile("xt", T, U16)
-        nc.scalar.dma_start(xt[:].bitcast(I32), xt_words[0].bitcast(I32))
+        nc.sync.dma_start(xt[:].bitcast(I32), xt_words[0].bitcast(I32))
+        l1 = load_list("l1", offs)
         w = tile("w", R, I32)
-        nc.scalar.dma_start(w[:], w_words[0].rearrange("p n t -> p (n t)").bitcast(I32))
+        nc.sync.dma_start(w[:], w_words[0].rearrange("p n t -> p (n t)").bitcast(I32))
+        w2_staged = load_staged("w2_staged", w2_scales, nc.sync)
+        l2 = load_list("l2", offs2)
+        l3 = load_list("l3", offs3)
         sa_t = tile("sa_t", PACK, F32)
         nc.gpsimd.dma_start(sa_t[:], sa.rearrange("(p t) o -> p (t o)", t=PACK))
         sb_t = tile("sb_t", PACK, F32)
         nc.gpsimd.dma_start(sb_t[:], sb.rearrange("(p t) o -> p (t o)", t=PACK))
-
-        l1 = load_list("l1", offs)
-        w_staged = load_staged("w_staged", w_scales)
-        load_plane(xt_plane, xt_scales)
+        ws = tile("ws", N, I32)
+        nc.gpsimd.dma_start(ws[:], ws_words[0].rearrange("p n t -> p (n t)").bitcast(I32))
+        wb = tile("wb", N, U16)
+        nc.gpsimd.dma_start(wb[:].bitcast(I32), wb_words[0].bitcast(I32))
         w2 = tile("w2", R, U16)
         nc.sync.dma_start(w2[:].bitcast(I32), w2_words[0].bitcast(I32))
         xo = tile("xo", Z, I32)
         nc.sync.dma_start(xo[:], xo_words[0].rearrange("p n t -> p (n t)").bitcast(I32))
-        l2 = load_list("l2", offs2)
-        w2_staged = load_staged("w2_staged", w2_scales)
-        load_plane(xo_plane, xo_scales)
-        l3 = load_list("l3", offs3)
         l5 = load_list("l5", offs5)
         l4 = load_list("l4", offs4)
-        ws = tile("ws", N, I32)
-        nc.sync.dma_start(ws[:], ws_words[0].rearrange("p n t -> p (n t)").bitcast(I32))
-        wb = tile("wb", N, U16)
-        nc.sync.dma_start(wb[:].bitcast(I32), wb_words[0].bitcast(I32))
-        load_plane(ws_plane, ws_scales)
-        load_plane(wb_plane, wb_scales)
+        load_plane(xo_plane, xo_scales, nc.sync)
+        load_plane(ws_plane, ws_scales, nc.sync)
+        load_plane(wb_plane, wb_scales, nc.sync)
 
         w_dealt = tile("w_dealt", R, U32)
         nc.scalar.copy(w_dealt[:].rearrange("p (t m) -> p m t", t=PACK), w[:].bitcast(U32).rearrange("p (m t) -> p m t", t=PACK))
+        spread(xt_plane, xt_staged)
         spread(w_plane, w_staged)
-        w_sc = deal_bytes("w_sc", w_plane)
         xt_sc = gather("xt_sc", xt_plane[:], l1, J, U8)
+        w_sc = deal_bytes("w_sc", w_plane)
         xt_g = gather("xt_g", xt[:], l1, J, U16)
         w2_dealt = tile("w2_dealt", R, U16)
         nc.scalar.copy(w2_dealt[:].rearrange("p (t m) -> p t m", t=PACK), w2[:].rearrange("p (m t) -> p t m", t=PACK))

@@ -46,9 +46,9 @@ def tile_list_weighedboth_twotab_further_plain_kernel(
             engine.memset(t[:].bitcast(I32), 0)
             return t
 
-        def load_plane(plane, scales, queue):
+        def load_plane(plane, scales, queue, quads=range(QUADS)):
             rows = scales[0].bitcast(I32)
-            for q in range(QUADS):
+            for q in quads:
                 queue.dma_start(plane[QUAD * q : QUAD * q + ROWS, :].bitcast(I32), rows[ROWS * q : ROWS * (q + 1), :])
 
         def load_staged(name, scales, queue):
@@ -71,47 +71,47 @@ def tile_list_weighedboth_twotab_further_plain_kernel(
             nc.vector.tensor_copy(t[:], window.indirect(offsets[:]))
             return t
 
-        xt_plane = zeroed_plane("xt_plane", T, nc.vector)
+        xt_plane = zeroed_plane("xt_plane", T, nc.gpsimd)
+        xo_plane = zeroed_plane("xo_plane", Z, nc.gpsimd)
         w_plane = zeroed_plane("w_plane", R, nc.vector)
-        xo_plane = zeroed_plane("xo_plane", Z, nc.vector)
         w2_plane = zeroed_plane("w2_plane", R, nc.vector)
         ws_plane = zeroed_plane("ws_plane", N, nc.vector)
         wb_plane = zeroed_plane("wb_plane", N, nc.vector)
 
-        xt_staged = load_staged("xt_staged", xt_scales, nc.sync)
         w_staged = load_staged("w_staged", w_scales, nc.sync)
         xt = tile("xt", T, U16)
         nc.sync.dma_start(xt[:].bitcast(I32), xt_words[0].bitcast(I32))
         l1 = load_list("l1", offs)
         w = tile("w", R, I32)
         nc.sync.dma_start(w[:], w_words[0].rearrange("p n t -> p (n t)").bitcast(I32))
-        w2_staged = load_staged("w2_staged", w2_scales, nc.sync)
-        l2 = load_list("l2", offs2)
-        l3 = load_list("l3", offs3)
+        load_plane(xt_plane, xt_scales, nc.sync)
+        load_plane(xo_plane, xo_scales, nc.gpsimd, range(QUADS - 1, QUADS))
         sa_t = tile("sa_t", PACK, F32)
         nc.gpsimd.dma_start(sa_t[:], sa.rearrange("(p t) o -> p (t o)", t=PACK))
         sb_t = tile("sb_t", PACK, F32)
         nc.gpsimd.dma_start(sb_t[:], sb.rearrange("(p t) o -> p (t o)", t=PACK))
-        ws = tile("ws", N, I32)
-        nc.gpsimd.dma_start(ws[:], ws_words[0].rearrange("p n t -> p (n t)").bitcast(I32))
-        wb = tile("wb", N, U16)
-        nc.gpsimd.dma_start(wb[:].bitcast(I32), wb_words[0].bitcast(I32))
+        w2_staged = load_staged("w2_staged", w2_scales, nc.sync)
         w2 = tile("w2", R, U16)
         nc.sync.dma_start(w2[:].bitcast(I32), w2_words[0].bitcast(I32))
         xo = tile("xo", Z, I32)
         nc.sync.dma_start(xo[:], xo_words[0].rearrange("p n t -> p (n t)").bitcast(I32))
+        l2 = load_list("l2", offs2)
+        l3 = load_list("l3", offs3)
+        load_plane(xo_plane, xo_scales, nc.sync, range(QUADS - 1))
         l5 = load_list("l5", offs5)
         l4 = load_list("l4", offs4)
-        load_plane(xo_plane, xo_scales, nc.sync)
+        ws = tile("ws", N, I32)
+        nc.sync.dma_start(ws[:], ws_words[0].rearrange("p n t -> p (n t)").bitcast(I32))
+        wb = tile("wb", N, U16)
+        nc.sync.dma_start(wb[:].bitcast(I32), wb_words[0].bitcast(I32))
         load_plane(ws_plane, ws_scales, nc.sync)
         load_plane(wb_plane, wb_scales, nc.sync)
 
         w_dealt = tile("w_dealt", R, U32)
         nc.scalar.copy(w_dealt[:].rearrange("p (t m) -> p m t", t=PACK), w[:].bitcast(U32).rearrange("p (m t) -> p m t", t=PACK))
-        spread(xt_plane, xt_staged)
         spread(w_plane, w_staged)
-        xt_sc = gather("xt_sc", xt_plane[:], l1, J, U8)
         w_sc = deal_bytes("w_sc", w_plane)
+        xt_sc = gather("xt_sc", xt_plane[:], l1, J, U8)
         xt_g = gather("xt_g", xt[:], l1, J, U16)
         w2_dealt = tile("w2_dealt", R, U16)
         nc.scalar.copy(w2_dealt[:].rearrange("p (t m) -> p t m", t=PACK), w2[:].rearrange("p (m t) -> p t m", t=PACK))

@@ -88,16 +88,17 @@ def tile_list_weighedboth_twotab_further_plain_kernel(
         load_plane(xo_plane, xo_scales, nc.gpsimd, range(QUADS - 1, QUADS))
         sa_t = tile("sa_t", PACK, F32)
         nc.gpsimd.dma_start(sa_t[:], sa.rearrange("(p t) o -> p (t o)", t=PACK))
+        load_plane(w2_plane, w2_scales, nc.gpsimd, range(QUADS - 1, QUADS))
         sb_t = tile("sb_t", PACK, F32)
         nc.gpsimd.dma_start(sb_t[:], sb.rearrange("(p t) o -> p (t o)", t=PACK))
-        w2_staged = load_staged("w2_staged", w2_scales, nc.sync)
         w2 = tile("w2", R, U16)
         nc.sync.dma_start(w2[:].bitcast(I32), w2_words[0].bitcast(I32))
+        l2 = load_list("l2", offs2)
         xo = tile("xo", Z, I32)
         nc.sync.dma_start(xo[:], xo_words[0].rearrange("p n t -> p (n t)").bitcast(I32))
-        l2 = load_list("l2", offs2)
         l3 = load_list("l3", offs3)
         load_plane(xo_plane, xo_scales, nc.sync, range(QUADS - 1))
+        load_plane(w2_plane, w2_scales, nc.sync, range(QUADS - 1))
         l5 = load_list("l5", offs5)
         l4 = load_list("l4", offs4)
         ws = tile("ws", N, I32)
@@ -124,10 +125,9 @@ def tile_list_weighedboth_twotab_further_plain_kernel(
                                 rhs=xt_g[:].bitcast(E2M1), rhs_scale=xt_sc[:], start=True, stop=True)
             a_ps.append(ps)
 
-        spread(w2_plane, w2_staged)
-        w2_sc = deal_bytes("w2_sc", w2_plane)
         xo_sc = gather("xo_sc", xo_plane[:], l2, J, U8)
         xo_g = gather("xo_g", xo[:].bitcast(U32), l2, J, U32)
+        w2_sc = deal_bytes("w2_sc", w2_plane)
 
         ga = sb_pool.tile([P, PACK, O], F32, name="ga")
         gb = sb_pool.tile([P, PACK, O], F32, name="gb")

from contextlib import ExitStack

import concourse.mybir as mybir

K, F, T, Z, J, R, O, N = 512, 512, 1024, 1024, 256, 512, 128, 256
FLOPS = 2 * (K * R * J + F * R * J + R * N * O + K * N * O)

F32 = mybir.dt.float32
BF16 = mybir.dt.bfloat16
I32 = mybir.dt.int32
U32 = mybir.dt.uint32
U16 = mybir.dt.uint16
U8 = mybir.dt.uint8
E4M3 = mybir.dt.float8_e4m3fn_x4
E5M2 = mybir.dt.float8_e5m2_x4
E2M1 = mybir.dt.float4_e2m1fn_x4
ACT = mybir.ActivationFunctionType
ALU = mybir.AluOpType

P = 128
PACK = 4
QUADS = 4
QUAD = 32
ROWS = 4


def tile_list_weighedboth_twotab_further_plain_kernel(
    tc, xt_words, xt_scales, w_words, w_scales, xo_words, xo_scales, w2_words, w2_scales, sa, sb,
    wb_words, wb_scales, ws_words, ws_scales, offs, offs2, offs3, offs4, offs5, out,
):
    nc = tc.nc
    with ExitStack() as ctx:
        sb_pool = ctx.enter_context(tc.tile_pool(name="sbuf", bufs=1))
        psum = ctx.enter_context(tc.psum_pool(name="psum", bufs=1))

        def tile(name, cols, dtype, parts=P):
            return sb_pool.tile([parts, cols], dtype, name=name, align_bytes=64)

        def load_list(name, src):
            t = sb_pool.tile(list(src.shape), U16, name=name)
            nc.sync.dma_start(t[:], src)
            return t

        def zeroed_plane(name, cols, engine):
            t = tile(name, cols, U8)
            engine.memset(t[:].bitcast(I32), 0)
            return t

        def load_plane(plane, scales, queue, quads=range(QUADS)):
            rows = scales[0].bitcast(I32)
            for q in quads:
                queue.dma_start(plane[QUAD * q : QUAD * q + ROWS, :].bitcast(I32), rows[ROWS * q : ROWS * (q + 1), :])

        def load_staged(name, scales, queue):
            cols = scales.shape[2] // 4
            t = sb_pool.tile([ROWS, QUADS, cols], I32, name=name)
            queue.dma_start(t[:], scales[0].bitcast(I32).rearrange("(q r) c -> r q c", r=ROWS))
            return t

        def spread(plane, staged):
            for q in range(QUADS):
                nc.vector.tensor_copy(plane[QUAD * q : QUAD * q + ROWS, :].bitcast(I32), staged[:, q, :])

        def deal_bytes(name, plane):
            t = tile(name, R, U8)
            nc.vector.tensor_copy(t[:].rearrange("p (t m) -> p t m", t=PACK), plane[:].rearrange("p (m t) -> p t m", t=PACK))
            return t

        def gather(name, window, offsets, n, dtype):
            t = tile(name, n, dtype)
            nc.vector.tensor_copy(t[:], window.indirect(offsets[:]))
            return t

        xt_plane = zeroed_plane("xt_plane", T, nc.gpsimd)
        xo_plane = zeroed_plane("xo_plane", Z, nc.gpsimd)
        w_plane = zeroed_plane("w_plane", R, nc.vector)
        w2_plane = zeroed_plane("w2_plane", R, nc.vector)
        ws_plane = zeroed_plane("ws_plane", N, nc.vector)
        wb_plane = zeroed_plane("wb_plane", N, nc.vector)

        w_staged = load_staged("w_staged", w_scales, nc.sync)
        xt = tile("xt", T, U16)
        nc.sync.dma_start(xt[:].bitcast(I32), xt_words[0].bitcast(I32))
        l1 = load_list("l1", offs)
        w = tile("w", R, I32)
        nc.sync.dma_start(w[:], w_words[0].rearrange("p n t -> p (n t)").bitcast(I32))
        load_plane(xt_plane, xt_scales, nc.sync)
        load_plane(xo_plane, xo_scales, nc.gpsimd, range(QUADS - 1, QUADS))
        sa_t = tile("sa_t", PACK, F32)
        nc.gpsimd.dma_start(sa_t[:], sa.rearrange("(p t) o -> p (t o)", t=PACK))
        load_plane(w2_plane, w2_scales, nc.gpsimd, range(QUADS - 1, QUADS))
        sb_t = tile("sb_t", PACK, F32)
        nc.gpsimd.dma_start(sb_t[:], sb.rearrange("(p t) o -> p (t o)", t=PACK))
        w2 = tile("w2", R, U16)
        nc.sync.dma_start(w2[:].bitcast(I32), w2_words[0].bitcast(I32))
        l2 = load_list("l2", offs2)
        xo = tile("xo", Z, I32)
        nc.sync.dma_start(xo[:], xo_words[0].rearrange("p n t -> p (n t)").bitcast(I32))
        l3 = load_list("l3", offs3)
        load_plane(xo_plane, xo_scales, nc.sync, range(QUADS - 1))
        load_plane(w2_plane, w2_scales, nc.sync, range(QUADS - 1))
        l5 = load_list("l5", offs5)
        l4 = load_list("l4", offs4)
        ws = tile("ws", N, I32)
        nc.sync.dma_start(ws[:], ws_words[0].rearrange("p n t -> p (n t)").bitcast(I32))
        wb = tile("wb", N, U16)
        nc.sync.dma_start(wb[:].bitcast(I32), wb_words[0].bitcast(I32))
        load_plane(ws_plane, ws_scales, nc.sync)
        load_plane(wb_plane, wb_scales, nc.sync)

        w_dealt = tile("w_dealt", R, U32)
        nc.scalar.copy(w_dealt[:].rearrange("p (t m) -> p m t", t=PACK), w[:].bitcast(U32).rearrange("p (m t) -> p m t", t=PACK))
        spread(w_plane, w_staged)
        w_sc = deal_bytes("w_sc", w_plane)
        xt_sc = gather("xt_sc", xt_plane[:], l1, J, U8)
        xt_g = gather("xt_g", xt[:], l1, J, U16)
        w2_dealt = tile("w2_dealt", R, U16)
        nc.scalar.copy(w2_dealt[:].rearrange("p (t m) -> p t m", t=PACK), w2[:].rearrange("p (m t) -> p t m", t=PACK))

        a_ps = []
        for t in range(PACK):
            cols = slice(P * t, P * (t + 1))
            ps = psum.tile([P, J], F32, name="a_ps%d" % t, tag="bank%d" % t)
            nc.tensor.matmul_mx(out=ps[:], lhsT=w_dealt[:, cols].bitcast(E4M3), lhsT_scale=w_sc[:, cols],
                                rhs=xt_g[:].bitcast(E2M1), rhs_scale=xt_sc[:], start=True, stop=True)
            a_ps.append(ps)

        xo_sc = gather("xo_sc", xo_plane[:], l2, J, U8)
        xo_g = gather("xo_g", xo[:].bitcast(U32), l2, J, U32)
        w2_sc = deal_bytes("w2_sc", w2_plane)

        ga = sb_pool.tile([P, PACK, O], F32, name="ga")
        gb = sb_pool.tile([P, PACK, O], F32, name="gb")
        a_sb = []
        for t in range(PACK):
            a_t = tile("a%d" % t, J, F32)
            nc.scalar.copy(a_t[:], a_ps[t][:])
            a_sb.append(a_t)
            if t > 0:
                nc.scalar.activation(out=ga[:, t - 1, :], in_=a_sb[t - 1][:].indirect(l3[:]), func=ACT.Copy, scale=sa_t[:, t - 1 : t])
        nc.scalar.activation(out=ga[:, PACK - 1, :], in_=a_sb[PACK - 1][:].indirect(l3[:]), func=ACT.Copy, scale=sa_t[:, PACK - 1 : PACK])

        b_ps = []
        for t in range(PACK):
            cols = slice(P * t, P * (t + 1))
            ps = psum.tile([P, J], F32, name="b_ps%d" % t, tag="bank%d" % (PACK + t))
            nc.tensor.matmul_mx(out=ps[:], lhsT=w2_dealt[:, cols].bitcast(E2M1), lhsT_scale=w2_sc[:, cols],
                                rhs=xo_g[:].bitcast(E4M3), rhs_scale=xo_sc[:], start=True, stop=True)
            b_ps.append(ps)

        x5_sc = gather("x5_sc", xt_plane[:], l5, O, U8)
        x5_g = gather("x5_g", xt[:], l5, O, U16)

        diff = sb_pool.tile([P, PACK, O], F32, name="diff")
        for t in range(PACK):
            b_t = tile("b%d" % t, J, F32)
            nc.vector.tensor_copy(b_t[:], b_ps[t][:])
            nc.scalar.activation(out=gb[:, t, :], in_=b_t[:].indirect(l4[:]), func=ACT.Copy, scale=sb_t[:, t : t + 1])

        y_ps = []
        for u in range(N // P):
            cols = slice(P * u, P * (u + 1))
            ps = psum.tile([P, O], F32, name="y_ps%d" % u, tag="bank%d" % u)
            nc.tensor.matmul_mx(out=ps[:], lhsT=ws[:, cols].bitcast(E4M3), lhsT_scale=ws_plane[:, cols],
                                rhs=x5_g[:].bitcast(E2M1), rhs_scale=x5_sc[:], start=True, stop=False)
            y_ps.append(ps)

        for t in range(PACK):
            nc.vector.tensor_tensor(diff[:, t, :], ga[:, t, :], gb[:, t, :], ALU.subtract)

        hid = sb_pool.tile([P, O, PACK], BF16, name="hid", align_bytes=64)
        diff_ot = diff[:].rearrange("p t o -> p o t")
        half = O // 2
        nc.vector.scalar_tensor_tensor(hid[:, :half, :], diff_ot[:, :half, :], -1.0, diff_ot[:, :half, :], ALU.mult, ALU.max)
        nc.scalar.activation(out=hid[:, half:, :], in_=diff_ot[:, half:, :], func=ACT.Abs)

        hid_q = tile("hid_q", O, U32)
        hid_sc = tile("hid_sc", O, U8)
        nc.vector.quantize_mx(out=hid_q[:].bitcast(E5M2), scales=hid_sc[:], in_=hid[:].rearrange("p o t -> p (o t)"))

        for u in range(N // P):
            cols = slice(P * u, P * (u + 1))
            nc.tensor.matmul_mx(out=y_ps[u][:], lhsT=wb[:, cols].bitcast(E2M1), lhsT_scale=wb_plane[:, cols],
                                rhs=hid_q[:].bitcast(E5M2), rhs_scale=hid_sc[:], start=False, stop=True)
        y0 = tile("y0", O, F32)
        nc.vector.tensor_copy(y0[:], y_ps[0][:])
        nc.sync.dma_start(out[0:P, :], y0[:])
        y1 = tile("y1", O, F32)
        nc.scalar.copy(y1[:], y_ps[1][:])
        nc.scalar.dma_start(out[P:N, :], y1[:])
